import numpy as np
import ml_dtypes


def mxq(x, axis, fmt="e4m3"):
    dtype, down = {"e4m3": (ml_dtypes.float8_e4m3fn, 7), "e5m2": (ml_dtypes.float8_e5m2, 14)}[fmt]
    v = np.moveaxis(np.asarray(x, np.float32).astype(ml_dtypes.bfloat16).astype(np.float64), axis, -1)
    blocks = v.reshape(v.shape[:-1] + (-1, 32))
    amax = np.abs(blocks).max(-1, keepdims=True)
    byte = np.maximum(np.where(amax > 0, np.frexp(amax)[1] - 1 + 127, 0) - down, 1)
    scale = np.exp2(byte - 127.0)
    codes = (blocks / scale).astype(np.float32).astype(dtype).astype(np.float64)
    return np.moveaxis((codes * scale).reshape(v.shape), -1, axis)


WIDE = False


def mx_kscale(k):
    if not WIDE:
        return np.ones(k)
    levels = np.array([10, -10, 5, -5, 0])
    if k % 512:
        return np.exp2(np.random.permutation(np.resize(levels, k // 32))).repeat(32)
    a = np.empty((k // 512, 16))
    for p in range(k // 512):
        a[p, :8] = np.random.permutation(np.resize(levels, 8))
        for g in range(8):
            far = levels[np.abs(levels - a[p, g]) >= 10]
            a[p, g + 8] = far[np.random.randint(len(far))]
    return np.exp2(a.ravel()).repeat(32)


BF16 = ml_dtypes.bfloat16


def bf(x):
    return np.asarray(x, np.float32).astype(BF16)


def f64(x):
    return np.asarray(x).astype(np.float64)


M, P, F, Q = 512, 1024, 1536, 1024


def soft(v, th):
    return np.sign(v) * np.maximum(np.abs(v) - th, 0.0)


def noise(*shape):
    return np.random.standard_normal(shape)


def draw0():
    s, r, w, t = mx_kscale(P), mx_kscale(F), mx_kscale(Q), mx_kscale(F)
    return {"x": bf(noise(M, P) * s),
            "enc": bf(noise(P, F) / np.sqrt(P) / s[:, None]),
            "z0": bf(soft(noise(M, F), 0.3) * r),
            "gram": bf(noise(F, F) / np.sqrt(F) / r[:, None]),
            "keep": bf((1 + 0.1 * noise(F)) * t / r),
            "step": bf(0.8 * (1 + 0.1 * noise(F)) * t),
            "theta": bf(0.3 * (1 + 0.1 * noise(F)) * t),
            "coef": bf(noise(F, Q) / np.sqrt(Q) * w),
            "base": bf(noise(Q, P) / w[:, None]),
            "gain": bf((1 + 0.1 * noise(F)) / t),
            "pix": bf((1 + 0.1 * noise(P)) / s)}


def core(x, enc, z0, gram, keep, step, theta, coef, base, gain, pix):
    u = mxq(f64(x), 1, "e4m3") @ mxq(f64(enc), 0, "e4m3")
    y = mxq(f64(z0), 1, "e4m3") @ mxq(f64(gram), 0, "e4m3")
    v = f64(keep) * f64(z0) + f64(step) * (u - y)
    z = soft(v, f64(theta))
    d = mxq(f64(coef), 1, "e4m3") @ mxq(f64(base), 0, "e4m3")
    length = np.sqrt(np.sum(d * d, axis=1, keepdims=True))
    atoms = d / length * f64(gain)[:, None]
    rec = mxq(z, 1, "e4m3") @ mxq(atoms, 0, "e4m3")
    res = f64(x) * f64(pix) - rec
    amp = z * f64(gain)
    return res, amp


def e4m3fn_bytes(y):
    return np.clip(np.asarray(y, np.float64), -448.0, 448.0).astype(np.float32).astype(ml_dtypes.float8_e4m3fn).view(np.uint8)


def e4m3fn_values(b):
    return np.asarray(b, np.uint8).view(ml_dtypes.float8_e4m3fn).astype(np.float64)


def setup_inputs():
    d = draw0()
    x0 = np.asarray(d['gram']).astype(np.float64)
    s = (np.max(np.abs(x0), axis=(1,), keepdims=True) / 448.0).astype(np.float32)
    out = {}
    for k, v in d.items():
        if k == 'gram':
            out['gram_bytes'] = e4m3fn_bytes(x0 / s.astype(np.float64))
            out['gram_scale'] = s
        else:
            out[k] = v
    return out


def reference(x, enc, z0, gram_bytes, gram_scale, keep, step, theta, coef, base, gain, pix):
    return core(x, enc, z0, e4m3fn_values(gram_bytes) * gram_scale.astype(np.float64), keep, step, theta, coef, base, gain, pix)

from contextlib import ExitStack

import concourse.mybir as mybir
from concourse.masks import make_identity

M, PIX, F, Q = 512, 1024, 1536, 1024
P = 128
PACK = 4
KP = 512
FLOPS = 2 * (M * PIX * F + M * F * F + F * Q * PIX + M * F * PIX)

F32 = mybir.dt.float32
BF16 = mybir.dt.bfloat16
U32 = mybir.dt.uint32
U8 = mybir.dt.uint8
FP8 = mybir.dt.float8_e4m3fn
FP8X4 = mybir.dt.float8_e4m3fn_x4
ALU = mybir.AluOpType
ACT = mybir.ActivationFunctionType

GF = F // KP
GX = PIX // KP
GQ = Q // KP
MT = M // P
B8 = 4
ST = 5


ORDER = [
    ("load","coef",0,),
    ("load","base",0,),
    ("load","base",1,),
    ("load","gram",0,0,),
    ("load","enc",0,0,),
    ("load","x",0,),
    ("load","x",1,),
    ("load","x",2,),
    ("load","x",3,),
    ("load","gram",0,1,),
    ("load","enc",0,1,),
    ("load","gram",0,2,),
    ("coef",0,0,),
    ("coef",0,1,),
    ("load","z0",0,),
    ("base",0,0,"t",),
    ("base",0,1,"t",),
    ("load","z0",1,),
    ("base",1,0,"t",),
    ("base",1,1,"t",),
    ("load","coef",1,),
    ("gs",),
    ("gram",0,0,),
    ("enc",0,0,"v",),
    ("load","gram",1,0,),
    ("load","enc",1,0,),
    ("load","gram",1,1,),
    ("vec",),
    ("norm",0,0,),
    ("x",0,),
    ("norm",0,1,),
    ("gram",0,1,),
    ("x",1,),
    ("norm",0,2,),
    ("enc",0,1,"v",),
    ("norm",0,3,),
    ("scale",0,),
    ("load","enc",1,1,),
    ("load","pix",),
    ("load","gram",1,2,),
    ("gram",0,2,),
    ("z0",0,),
    ("load","gram",2,0,),
    ("load","coef",2,),
    ("z0",1,),
    ("coef",1,0,),
    ("z0",2,),
    ("coef",1,1,),
    ("atoms",0,0,0,),
    ("atoms",0,0,1,),
    ("atoms",0,1,0,),
    ("atoms",0,1,1,),
    ("w",0,0,),
    ("gram",1,0,),
    ("load","enc",2,0,),
    ("w",0,1,),
    ("held",1,0,),
    ("w",0,2,),
    ("enc",1,0,"v",),
    ("load","gram",2,1,),
    ("w",0,3,),
    ("held",1,1,),
    ("z",0,),
    ("gram",1,1,),
    ("load","enc",2,1,),
    ("gained",0,"v",),
    ("held",1,2,),
    ("amp",0,0,"s",),
    ("enc",1,1,"v",),
    ("load","gram",2,2,),
    ("amp",0,1,"s",),
    ("held",1,3,),
    ("amp",0,2,"s",),
    ("gram",1,2,),
    ("amp",0,3,"s",),
    ("coef",2,0,),
    ("coef",2,1,),
    ("join",1,0,"v",),
    ("join",1,1,"v",),
    ("w",1,0,),
    ("gram",2,0,),
    ("w",1,1,),
    ("held",2,0,),
    ("w",1,2,),
    ("enc",2,0,"v",),
    ("w",1,3,),
    ("held",2,1,),
    ("z",1,),
    ("gram",2,1,),
    ("gained",1,"v",),
    ("held",2,2,),
    ("amp",1,0,"s",),
    ("enc",2,1,"v",),
    ("amp",1,1,"s",),
    ("held",2,3,),
    ("amp",1,2,"s",),
    ("gram",2,2,),
    ("amp",1,3,"s",),
    ("join",2,0,"v",),
    ("join",2,1,"v",),
    ("w",2,0,),
    ("w",2,1,),
    ("load","xin",0,0,),
    ("xp",0,0,),
    ("load","xin",0,1,),
    ("xp",0,1,),
    ("w",2,2,),
    ("w",2,3,),
    ("z",2,),
    ("load","xin",0,2,),
    ("xp",0,2,),
    ("load","xin",0,3,),
    ("xp",0,3,),
    ("res",0,0,),
    ("load","xin",1,0,),
    ("xp",1,0,),
    ("res",0,1,),
    ("load","xin",1,1,),
    ("xp",1,1,),
    ("res",0,2,),
    ("load","xin",1,2,),
    ("xp",1,2,),
    ("res",0,3,),
    ("load","xin",1,3,),
    ("xp",1,3,),
    ("gained",2,"v",),
    ("res",1,0,),
    ("amp",2,0,"s",),
    ("res",1,1,),
    ("amp",2,1,"s",),
    ("res",1,2,),
    ("amp",2,2,"s",),
    ("res",1,3,),
    ("amp",2,3,"s",),
]


def tile_dictionary_ista_step_f5_kernel(
    tc, x, enc, z0, gram_bytes, gram_scale, keep, step, theta, coef, base, gain, pix, res, amp
):
    nc = tc.nc
    with ExitStack() as ctx:
        one = ctx.enter_context(tc.tile_pool(name="one", bufs=1))
        pool = ctx.enter_context(tc.tile_pool(name="pool", bufs=2))
        psum = ctx.enter_context(tc.psum_pool(name="psum", bufs=8))


        def sb(shape, dtype, tag, bufs):
            return pool.tile(shape, dtype, name=tag, tag=tag, bufs=bufs, align_bytes=64)

        def bank(shape, dtype):
            return psum.tile(shape, dtype, name="bank", tag="bank", bufs=8)

        def quantize(src, tag, bufs):
            c = sb([P, KP], U32, tag + "_c", bufs)
            s = sb([P, KP], U8, tag + "_s", bufs)
            nc.vector.quantize_mx(out=c[:].bitcast(FP8X4), scales=s[:], in_=src[:].rearrange("p n j -> p (n j)"))
            return c, s

        def mx(ps, l, lc, r, rc, first, last):
            nc.tensor.matmul_mx(
                out=ps,
                lhsT=l[0][:, lc].bitcast(FP8X4),
                lhsT_scale=l[1][:, lc],
                rhs=r[0][:, rc].bitcast(FP8X4),
                rhs_scale=r[1][:, rc],
                start=first,
                stop=last,
            )

        raw = {}

        def load_rows(name, src, g, tag, bufs):
            t_ = sb([P, PACK, src.shape[1]], BF16, tag, bufs)
            nc.sync.dma_start(out=t_[:], in_=src.rearrange("(g p j) n -> g p j n", p=P, j=PACK)[g])
            raw[name, g] = t_

        def load_block(name, src, dtype, g, k, bufs):
            t_ = sb([P, PACK, KP], dtype, name + "_raw", bufs)
            nc.sync.dma_start(
                out=t_[:], in_=src.rearrange("(k p j) n -> k p j n", p=P, j=PACK)[k][:, :, g * KP : (g + 1) * KP]
            )
            raw[name, g, k] = t_

        def load_gram(g, k):
            load_block("gram", gram_bytes, U8, g, k, 4)

        def load_enc(g, k):
            load_block("enc", enc, BF16, g, k, 3)

        gs = one.tile([P, GF, PACK], F32, name="gs")
        nc.scalar.dma_start(out=gs[:], in_=gram_scale.rearrange("(g p t) o -> p g (t o)", p=P, t=PACK))
        vec_b = one.tile([P, 4, 16], BF16, name="vec_b")
        for i, v in enumerate((keep, step, theta, gain)):
            nc.scalar.dma_start(
                out=vec_b[:, i, 0:12].rearrange("p (g t) -> p g t", t=PACK),
                in_=v.rearrange("(g p t) -> p g t", p=P, t=PACK),
            )
        gain_bc = one.tile([P, F], BF16, name="gain_bc")
        pix_bc = one.tile([P, PIX], BF16, name="pix_bc")

        ident_f = one.tile([P, P], F32, name="ident_f")
        make_identity(nc, ident_f[:])
        ident_b = one.tile([P, P], BF16, name="ident_b")
        make_identity(nc, ident_b[:])


        vec = one.tile([P, 4, 12], F32, name="vec")
        ntheta = one.tile([P, 12], F32, name="ntheta")
        ngs = one.tile([P, GF, PACK], F32, name="ngs")
        ss = one.tile([P, 2, 12], F32, name="ss")
        keep_v, step_v, theta_v, gain_v = [vec[:, i, :] for i in range(4)]

        def prep_gs():
            nc.vector.tensor_scalar(out=ngs[:], in0=gs[:], scalar1=-1.0, scalar2=None, op0=ALU.mult)

        def prep_vec():
            nc.vector.tensor_copy(out=vec[:], in_=vec_b[:, :, 0:12])
            nc.vector.tensor_scalar(out=ntheta[:], in0=theta_v, scalar1=-1.0, scalar2=None, op0=ALU.mult)

        codes = {}

        def turn_unit(rows, k, key, bufs, eng, tag="st4", gbufs=ST, keep_as=None):
            box = {}

            def turn(h):
                ps = box["ps", h] = bank([P, 2, 2, P], F32)
                for i in range(2):
                    words = rows[2 * h + i].bitcast(F32)
                    for u in range(2):
                        nc.tensor.transpose(ps[:, i, u, :], words[:, 256 * k + u : 256 * (k + 1) : 2], ident_f[:])

            def out(h, eng):
                if h == 0:
                    box["gr"] = sb([P, KP, PACK], BF16, tag, gbufs)
                    if keep_as is not None:
                        codes[keep_as] = box["gr"]
                dst = box["gr"][:, 256 * h : 256 * (h + 1), :].rearrange("p r j -> p (r j)").bitcast(F32)
                cp = nc.scalar.copy if eng == "s" else nc.vector.tensor_copy
                cp(
                    out=dst.rearrange("p (i r u) -> p i r u", i=2, u=2),
                    in_=box["ps", h][:].rearrange("p i u r -> p i r u"),
                )

            def s0():
                turn(0)
                turn(1)

            def s1():
                out(0, eng[0])
                out(1, eng[1])

            def s2():
                codes[key] = quantize(box["gr"], key[0], bufs)

            return [s0, s1, s2]

        def x_unit(k, eng="ss"):
            return turn_unit([raw["x"][:, a, :] for a in range(MT)], k, ("x", k), 2, eng)

        def z0_unit(k, eng="ss"):
            return turn_unit([raw["z0", a // 2][:, a % 2, :] for a in range(MT)], k, ("z0", k), 3, eng, "z0g", 3, ("z0g", k))

        def coef_unit(g, q, eng="ss"):
            return turn_unit([raw["coef", g][:, t, :] for t in range(PACK)], q, ("coef", g, q), 4, eng)

        def inter_v(src, key, bufs):
            box = {}

            def s0():
                box["il"] = sb([P, KP, PACK], BF16, "st4", ST)
                nc.vector.tensor_copy(out=box["il"][:].rearrange("p (t m) j -> p t m j", t=PACK), in_=src())

            def s1():
                codes[key] = quantize(box["il"], key[0], bufs)

            return [s0, s1]

        def inter_t(src, key, bufs):
            box = {}

            def s0():
                for e in range(2):
                    ps = box[e] = bank([P, 2, 128, PACK], BF16)
                    for s in range(2):
                        nc.tensor.matmul(
                            ps[:, s, :, :], lhsT=ident_b[:], rhs=src()[:, 2 * e + s, :, :], start=True, stop=True
                        )

            def s1():
                box["il"] = sb([P, KP, PACK], BF16, "st4", ST)
                for e in range(2):
                    nc.scalar.copy(
                        out=box["il"][:, 256 * e : 256 * (e + 1), :].rearrange("p n j -> p (n j)"),
                        in_=box[e][:].rearrange("p s n j -> p (s n j)"),
                    )

            def s2():
                codes[key] = quantize(box["il"], key[0], bufs)

            return [s0, s1, s2]

        def base_unit(q, h, mode):
            def src():
                return raw["base", q][:, :, KP * h : KP * (h + 1)].rearrange("p j (t m) -> p t m j", t=PACK)

            return (inter_t if mode == "t" else inter_v)(src, ("base", q, h), 4)

        def enc_unit(g, k, mode):
            def src():
                return raw["enc", g, k][:].rearrange("p j (m t) -> p t m j", t=PACK)

            return (inter_t if mode == "t" else inter_v)(src, ("enc", g, k), 4)

        def gram_unit(g, k, mode="v"):
            box = {}

            def s0():
                box["wide"] = sb([P, PACK, KP], BF16, "wide", 3)
                for j in range(PACK):
                    nc.scalar.activation(
                        out=box["wide"][:, j, :],
                        in_=raw["gram", g, k][:, j, :].bitcast(FP8),
                        func=ACT.Copy,
                        scale=ngs[:, k, j : j + 1],
                    )

            def src():
                return box["wide"][:].rearrange("p j (m t) -> p t m j", t=PACK)

            return [s0] + (inter_t if mode == "t" else inter_v)(src, ("gram", g, k), 6)

        def norm_unit(g, t, box=None):
            box = {} if box is None else box
            c = PACK * g + t

            def s0():
                for h in range(2):
                    ps = box[h] = bank([P, KP], F32)
                    for q in range(GQ):
                        mx(
                            ps[:],
                            codes["coef", g, q],
                            slice(P * t, P * (t + 1)),
                            codes["base", q, h],
                            slice(0, KP),
                            q == 0,
                            q == GQ - 1,
                        )

            def s1():
                for h in range(2):
                    junk = sb([P, KP], BF16, "junk", 1)
                    nc.scalar.activation(out=junk[:], in_=box[h][:], func=ACT.Square, accum_out=ss[:, h, c : c + 1])

            return [s0, s1]

        def scale_unit(g):
            cs = slice(PACK * g, PACK * (g + 1))
            box = {}

            def s0():
                box["tot"] = sb([P, PACK], F32, "tot", 2)
                nc.vector.tensor_add(out=box["tot"][:], in0=ss[:, 0, cs], in1=ss[:, 1, cs])

            def s1():
                box["root"] = sb([P, PACK], F32, "root", 2)
                nc.scalar.activation(out=box["root"][:], in_=box["tot"][:], func=ACT.Sqrt)

            def s2():
                inv = sb([P, PACK], F32, "inv", 2)
                nc.vector.reciprocal(out=inv[:], in_=box["root"][:])
                codes["scale", g] = sb([P, PACK], F32, "scale", 3)
                nc.vector.tensor_mul(out=codes["scale", g][:], in0=inv[:], in1=gain_v[:, cs])

            return [s0, s1, s2]

        abox = {}

        def atoms_unit(g, h, part):
            box = abox.setdefault((g, h), {})

            def t_(b):
                def f():
                    ps = box[b] = bank([P, PACK, P], F32)
                    for t in range(PACK):
                        for q in range(GQ):
                            mx(
                                ps[:, t, :],
                                codes["coef", g, q],
                                slice(P * t, P * (t + 1)),
                                codes["base", q, h],
                                slice(P * b, P * (b + 1)),
                                q == 0,
                                q == GQ - 1,
                            )

                return f

            def v_(b):
                def f():
                    if b == 0:
                        box["at"] = sb([P, KP, PACK], BF16, "st4", ST)
                    nc.vector.tensor_tensor(
                        out=box["at"][:, P * b : P * (b + 1), :],
                        in0=box[b][:].rearrange("p t n -> p n t"),
                        in1=codes["scale", g][:].unsqueeze(1).to_broadcast([P, P, PACK]),
                        op=ALU.mult,
                    )

                return f

            def q_():
                codes["at", g, h] = quantize(box["at"], "at", 6)

            def both(*fs):
                def f():
                    for e in fs:
                        e()

                return f

            if part == 0:
                return [both(t_(0), t_(1)), both(v_(0), v_(1))]
            return [both(t_(2), t_(3)), both(v_(2), v_(3)), q_]

        def held_unit(g, t):
            box = {}
            c = PACK * g + t
            base_stages = norm_unit(g, t, box)

            def s2():
                root = box["root"] = sb([P, 1], F32, "hroot", 3)
                nc.scalar.activation(
                    out=root[:], in_=ss[:, 0, c : c + 1], func=ACT.Sqrt, bias=ss[:, 1, c : c + 1]
                )

            def s3():
                inv = sb([P, 1], F32, "hinv", 3)
                nc.vector.reciprocal(out=inv[:], in_=box["root"][:])
                box["sc"] = sb([P, 1], F32, "hsc", 3)
                nc.vector.tensor_mul(out=box["sc"][:], in0=inv[:], in1=gain_v[:, c : c + 1])

            def s4():
                if t == 0:
                    codes["planes", g] = [sb([P, PACK, KP], BF16, "wide", 3) for h in range(2)]
                for h in range(2):
                    nc.scalar.activation(
                        out=codes["planes", g][h][:, t, :], in_=box[h][:], func=ACT.Copy, scale=box["sc"][:]
                    )

            return [base_stages[0], lambda: (base_stages[1](), s2()), s3, s4]

        def held_join(g, h, eng="v"):
            box = {}

            def s0():
                box["at"] = sb([P, KP, PACK], BF16, "st4", ST)
                (nc.vector.tensor_copy if eng == "v" else nc.scalar.copy)(
                    out=box["at"][:], in_=codes["planes", g][h][:].rearrange("p t n -> p n t")
                )

            def s1():
                codes["at", g, h] = quantize(box["at"], "at", 6)

            return [s0, s1]

        def shrink_unit(g, t, eng="s", keng="s"):
            c = PACK * g + t
            cols = slice(P * t, P * (t + 1))
            box = {}

            def s0():
                ps = box["ps"] = bank([P, M], F32)
                for k in range(GX):
                    mx(ps[:], codes["enc", g, k], cols, codes["x", k], slice(0, M), k == 0, False)
                for k in range(GF):
                    mx(ps[:], codes["gram", g, k], cols, codes["z0", k], slice(0, M), False, k == GF - 1)
                box["kz"] = sb([P, M], F32, "kz", 2)
                if keng == "s":
                    nc.scalar.activation(
                        out=box["kz"][:], in_=codes["z0g", g][:, :, t], func=ACT.Copy, scale=keep_v[:, c : c + 1]
                    )
                elif keng == "v":
                    nc.vector.tensor_scalar(
                        out=box["kz"][:],
                        in0=codes["z0g", g][:, :, t],
                        scalar1=keep_v[:, c : c + 1],
                        scalar2=None,
                        op0=ALU.mult,
                    )
                else:
                    nc.gpsimd.tensor_scalar(
                        out=box["kz"][:],
                        in0=codes["z0g", g][:, :, t],
                        scalar1=keep_v[:, c : c + 1],
                        scalar2=0.0,
                        op0=ALU.mult,
                        op1=ALU.add,
                    )

            def s1():
                box["v"] = sb([P, M], F32, "v", 2)
                nc.vector.scalar_tensor_tensor(
                    out=box["v"][:],
                    in0=box["ps"][:],
                    scalar=step_v[:, c : c + 1],
                    in1=box["kz"][:],
                    op0=ALU.mult,
                    op1=ALU.add,
                )

            def s2():
                box["r"] = sb([P, M], F32, "r", 2)
                if eng == "s":
                    nc.scalar.activation(out=box["r"][:], in_=box["v"][:], func=ACT.Relu, bias=ntheta[:, c : c + 1])
                else:
                    nc.vector.tensor_scalar(
                        out=box["r"][:],
                        in0=box["v"][:],
                        scalar1=ntheta[:, c : c + 1],
                        scalar2=0.0,
                        op0=ALU.add,
                        op1=ALU.max,
                    )

            def s3():
                if t == 0:
                    codes["zf", g] = sb([P, PACK, M], F32, "z8k", 2)
                nc.vector.scalar_tensor_tensor(
                    out=codes["zf", g][:, t, :],
                    in0=box["v"][:],
                    scalar=theta_v[:, c : c + 1],
                    in1=box["r"][:],
                    op0=ALU.add,
                    op1=ALU.min,
                )

            return [s0, s1, s2, s3]

        def z_unit(g, eng="v"):
            box = {}

            def s0():
                box["zb"] = sb([P, M, PACK], BF16, "st4", ST)
                (nc.vector.tensor_copy if eng == "v" else nc.scalar.copy)(out=box["zb"][:], in_=codes["zf", g][:].rearrange("p t m -> p m t"))

            def s1():
                codes["z", g] = quantize(box["zb"], "z", 3)

            return [s0, s1]

        def gained_unit(g, eng):
            def s0():
                for t in range(PACK):
                    c = PACK * g + t
                    if eng == "v":
                        nc.vector.tensor_scalar(
                            out=codes["zf", g][:, t, :],
                            in0=codes["zf", g][:, t, :],
                            scalar1=gain_v[:, c : c + 1],
                            scalar2=None,
                            op0=ALU.mult,
                        )
                    else:
                        nc.scalar.activation(
                            out=codes["zf", g][:, t, :],
                            in_=codes["zf", g][:, t, :],
                            func=ACT.Copy,
                            scale=gain_v[:, c : c + 1],
                        )

            return [s0]

        def amp_unit(g, a, mode="v"):
            box = {}

            def s0():
                src = codes["zf", g]
                ps = box["ps"] = bank([P, PACK, P], F32)
                for t in range(PACK):
                    nc.tensor.transpose(ps[:, t, :], src[:, t, P * a : P * (a + 1)], ident_f[:])

            def s1():
                o = sb([P, P, PACK], F32, "outs", 4)
                if mode == "v":
                    nc.vector.tensor_tensor(
                        out=o[:],
                        in0=box["ps"][:].rearrange("m t p -> m p t"),
                        in1=gain_bc[:, KP * g : KP * (g + 1)].rearrange("m (p t) -> m p t", t=PACK),
                        op=ALU.mult,
                    )
                else:
                    nc.scalar.copy(out=o[:], in_=box["ps"][:].rearrange("m t p -> m p t"))
                nc.sync.dma_start(
                    out=amp[P * a : P * (a + 1), KP * g : KP * (g + 1)], in_=o[:].rearrange("m p t -> m (p t)")
                )

            return [s0, s1]

        xp = {}

        def xp_unit(h, a, eng="g"):
            def s0():
                hs = slice(KP * h, KP * (h + 1))
                xp[h, a] = sb([P, KP], F32, "xp", 4)
                e = nc.gpsimd if eng == "g" else nc.vector
                e.tensor_tensor(out=xp[h, a][:], in0=raw["xin", h, a][:], in1=pix_bc[:, hs], op=ALU.mult)

            return [s0]

        def res_unit(h, a):
            box = {}

            def s0():
                ps = box["ps"] = bank([P, KP], F32)
                for g in range(GF):
                    mx(ps[:], codes["z", g], slice(P * a, P * (a + 1)), codes["at", g, h], slice(0, KP), g == 0, g == GF - 1)

            def s1():
                if ("out", h) not in codes:
                    codes["out", h] = sb([P, MT, KP], F32, "b8k", B8)
                o = codes["out", h][:, a, :]
                nc.vector.tensor_tensor(out=o, in0=xp[h, a][:], in1=box["ps"][:], op=ALU.subtract)
                nc.sync.dma_start(out=res[P * a : P * (a + 1), KP * h : KP * (h + 1)], in_=o)

            return [s0, s1]

        def load_unit(name, *args):
            def s0():
                if name == "x":
                    a = args[0]
                    if a == 0:
                        raw["x"] = sb([P, MT, PIX], BF16, "b8k", B8)
                    nc.sync.dma_start(out=raw["x"][:, a, :], in_=x[P * a : P * (a + 1), :])
                elif name == "xin":
                    h, a = args
                    raw["xin", h, a] = sb([P, KP], BF16, "xin", 3)
                    nc.sync.dma_start(
                        out=raw["xin", h, a][:], in_=x[P * a : P * (a + 1), KP * h : KP * (h + 1)]
                    )
                elif name == "z0":
                    b = args[0]
                    raw["z0", b] = sb([P, 2, F], BF16, "b8k", B8)
                    nc.sync.dma_start(
                        out=raw["z0", b][:], in_=z0[2 * P * b : 2 * P * (b + 1), :].rearrange("(a p) k -> p a k", p=P)
                    )
                elif name == "coef":
                    load_rows("coef", coef, args[0], "b8k", B8)
                elif name == "base":
                    load_rows("base", base, args[0], "b8k", B8)
                elif name == "enc":
                    load_enc(*args)
                elif name == "gram":
                    load_gram(*args)
                elif name == "gain":
                    nc.sync.dma_start(out=gain_bc[:], in_=gain.partition_broadcast(P))
                else:
                    nc.sync.dma_start(out=pix_bc[:], in_=pix.partition_broadcast(P))

            return [s0]

        def run(units):
            for u in units:
                for stage in u:
                    stage()

        def lazy(maker, *args):
            box = []

            def stage(s):
                def f():
                    if not box:
                        box.append(maker(*args))
                    if s < len(box[0]):
                        box[0][s]()

                return f

            return [stage(s) for s in range(4)]

        makers = {
            "gs": lambda: [prep_gs],
            "vec": lambda: [prep_vec],
            "load": load_unit,
            "gram": gram_unit,
            "enc": enc_unit,
            "base": base_unit,
            "x": x_unit,
            "z0": z0_unit,
            "coef": coef_unit,
            "norm": norm_unit,
            "scale": scale_unit,
            "atoms": atoms_unit,
            "held": held_unit,
            "join": held_join,
            "w": shrink_unit,
            "z": z_unit,
            "gained": gained_unit,
            "amp": amp_unit,
            "xp": xp_unit,
            "res": res_unit,
        }
        run([lazy(makers[u[0]], *u[1:]) for u in ORDER])
